import numpy as np
import ml_dtypes


def mxq(x, axis, fmt="e4m3"):
    dtype, down = {"e4m3": (ml_dtypes.float8_e4m3fn, 7), "e5m2": (ml_dtypes.float8_e5m2, 14)}[fmt]
    v = np.moveaxis(np.asarray(x, np.float32).astype(ml_dtypes.bfloat16).astype(np.float64), axis, -1)
    blocks = v.reshape(v.shape[:-1] + (-1, 32))
    amax = np.abs(blocks).max(-1, keepdims=True)
    byte = np.maximum(np.where(amax > 0, np.frexp(amax)[1] - 1 + 127, 0) - down, 1)
    scale = np.exp2(byte - 127.0)
    codes = (blocks / scale).astype(np.float32).astype(dtype).astype(np.float64)
    return np.moveaxis((codes * scale).reshape(v.shape), -1, axis)


WIDE = False


def mx_kscale(k):
    if not WIDE:
        return np.ones(k)
    levels = np.array([10, -10, 5, -5, 0])
    if k % 512:
        return np.exp2(np.random.permutation(np.resize(levels, k // 32))).repeat(32)
    a = np.empty((k // 512, 16))
    for p in range(k // 512):
        a[p, :8] = np.random.permutation(np.resize(levels, 8))
        for g in range(8):
            far = levels[np.abs(levels - a[p, g]) >= 10]
            a[p, g + 8] = far[np.random.randint(len(far))]
    return np.exp2(a.ravel()).repeat(32)


BF16 = ml_dtypes.bfloat16


def bf(x):
    return np.asarray(x, np.float32).astype(BF16)


def f64(x):
    return np.asarray(x).astype(np.float64)


E2M1 = np.array([0.0, 0.5, 1.0, 1.5, 2.0, 3.0, 4.0, 6.0, -0.0, -0.5, -1.0, -1.5, -2.0, -3.0, -4.0, -6.0])


def pack_weight(w, fmt):
    k, n = w.shape
    w = f64(bf(w)).reshape(k // 32, 32, n)
    amax = np.abs(w).max(1)
    if fmt == "e4m3":
        byte = np.frexp(amax)[1] - 1 + 127 - 7
    else:
        mant, ex = np.frexp(amax / 6.0)
        byte = np.where(mant > 0.5, ex, ex - 1) + 127
    byte = np.clip(np.where(amax > 0, byte, 1), 1, 254)
    scaled = (w * np.exp2(127.0 - byte)[:, None, :]).reshape(k, n).astype(np.float32)
    by_word = np.ascontiguousarray(scaled.reshape(k // 512, 128, 4, n).transpose(0, 1, 3, 2))
    if fmt == "e4m3":
        words = by_word.astype(ml_dtypes.float8_e4m3fn).view(np.uint8)
    else:
        c = by_word.astype(ml_dtypes.float4_e2m1fn).view(np.uint8) & 0xF
        words = c[..., 0::2] | (c[..., 1::2] << 4)
    return np.ascontiguousarray(words), np.ascontiguousarray(byte.astype(np.uint8).reshape(k // 512, 16, n))


def unpack_weight(words, scales, fmt):
    g, p, n, _ = words.shape
    if fmt == "e4m3":
        vals = np.ascontiguousarray(words).view(ml_dtypes.float8_e4m3fn).astype(np.float64)
    else:
        nib = np.empty((g, p, n, 4), np.uint8)
        nib[..., 0::2] = words & 0xF
        nib[..., 1::2] = words >> 4
        vals = E2M1[nib]
    vals = vals * np.repeat(np.exp2(scales.astype(np.float64) - 127.0), 8, axis=1)[..., None]
    return vals.transpose(0, 1, 3, 2).reshape(g * 512, n)
def pack4(w):
    words, scales = pack_weight(w, "e2m1")
    return words.reshape(words.shape[0], 128, -1), scales


def unpack4(words, scales):
    return unpack_weight(words.reshape(words.shape[0], 128, -1, 2), scales, "e2m1")


T, K, B, A, P = 2048, 1024, 1024, 512, 512

CAP_MEAN, CAP_SPREAD = 1.2, 0.1
GAIN_BASE = 0.3
COUPLING = 0.25


def setup_inputs():
    s = mx_kscale(K)
    v = mx_kscale(A)
    t = mx_kscale(B)
    weather = np.random.standard_normal((T, K)) * s
    response = np.random.standard_normal((K, B)) / np.sqrt(K) / s[:, None] * t
    base = GAIN_BASE * np.random.standard_normal(B) * t
    cap = (CAP_MEAN + CAP_SPREAD * np.random.standard_normal(B)) * t
    site = np.random.standard_normal((A, B)) * v[:, None] / t
    plant = COUPLING * np.random.standard_normal((A, P)) / np.sqrt(A) / v[:, None]
    site_words, site_scales = pack4(site)
    plant_words, plant_scales = pack4(plant)
    return {"weather": bf(weather), "response": bf(response), "base": bf(base), "cap": bf(cap),
            "site_words": site_words, "site_scales": site_scales,
            "plant_words": plant_words, "plant_scales": plant_scales}


def reference(weather, response, base, cap, site_words, site_scales, plant_words, plant_scales):
    raw = mxq(f64(weather), 1, "e4m3") @ mxq(f64(response), 0, "e4m3")
    load = np.minimum(np.maximum(raw + f64(base), 0.0), f64(cap))
    site = unpack4(site_words, site_scales)
    plant = unpack4(plant_words, plant_scales)
    coef = site.T @ plant
    return mxq(load, 1, "e4m3") @ mxq(coef, 0, "e4m3")

@@ -1,0 +1,386 @@
+from contextlib import ExitStack
+
+import concourse.mybir as mybir
+from concourse.masks import make_identity
+
+T, K, B, A, NP = 2048, 1024, 1024, 512, 512
+FLOPS = 2 * T * K * B + 2 * A * B * NP + 2 * T * B * NP
+
+F32 = mybir.dt.float32
+BF16 = mybir.dt.bfloat16
+U32 = mybir.dt.uint32
+I32 = mybir.dt.int32
+U8 = mybir.dt.uint8
+FP8X4 = mybir.dt.float8_e4m3fn_x4
+FP4X4 = mybir.dt.float4_e2m1fn_x4
+ALU = mybir.AluOpType
+ACT = mybir.ActivationFunctionType
+
+P = 128
+PACK = 4
+PASS = P * PACK
+CHUNK = 512
+HALF = 256
+CHUNKS = T // CHUNK
+BANKS = 8
+ALL = slice(0, CHUNK)
+HALVES = (slice(0, HALF), slice(HALF, CHUNK))
+
+
+def tile_district_heat_dispatch_s12_kernel(
+    tc, weather, response, base, cap, site_words, site_scales, plant_words, plant_scales, out
+):
+    nc = tc.nc
+    with ExitStack() as ctx:
+        keep = ctx.enter_context(tc.tile_pool(name="keep", bufs=1))
+        work = ctx.enter_context(tc.tile_pool(name="work", bufs=3))
+        psum = ctx.enter_context(tc.psum_pool(name="psum", bufs=1))
+        ctx.enter_context(tc.manual_schedule())
+
+        free_banks = list(range(BANKS))
+        number = {}
+
+        def take_bank(key):
+            number[key] = free_banks.pop(0)
+            return psum.tile([P, CHUNK], F32, name="bank%d" % number[key], tag="bank%d" % number[key])
+
+        def give_bank(key):
+            free_banks.append(number[key])
+
+        def copy_on(engine, dst, src):
+            if engine == "scalar":
+                nc.scalar.copy(out=dst, in_=src)
+            else:
+                nc.vector.tensor_copy(out=dst, in_=src)
+
+        def mx_tiles(name):
+            codes = keep.tile([P, CHUNK], U32, name=name + "_codes", align_bytes=64)
+            scales = keep.tile([P, CHUNK], U8, name=name + "_scales", align_bytes=64)
+            return codes, scales
+
+        def quantize(planes, grouped, cols=ALL):
+            nc.vector.quantize_mx(
+                out=planes[0][:, cols].bitcast(FP8X4),
+                scales=planes[1][:, cols],
+                in_=grouped[:, PACK * cols.start : PACK * cols.stop],
+            )
+
+        def grouped_tile(name):
+            return work.tile([P, PACK * CHUNK], BF16, name=name, tag="grouped", bufs=4, align_bytes=64)
+
+        def interleave(engine, grouped, slots, cols=ALL):
+            copy_on(
+                engine,
+                grouped[:, PACK * cols.start : PACK * cols.stop].rearrange("p (c i t) -> p c t i", i=4, t=PACK),
+                slots[:, :, cols].rearrange("p t (c i) -> p c t i", i=4),
+            )
+
+        w_raw, r_raw = {}, {}
+
+        def load_weather(h):
+            w_raw[h] = keep.tile([P, 2, K], BF16, name="w_raw%d" % h, align_bytes=64)
+            nc.sync.dma_start(
+                out=w_raw[h][:], in_=weather[HALF * h : HALF * (h + 1), :].rearrange("(n e) k -> n e k", e=2)
+            )
+
+        def load_response(g, s):
+            r_raw[g, s] = keep.tile([P, PACK, PASS], BF16, name="r_raw%d%d" % (g, s))
+            nc.sync.dma_start(
+                out=r_raw[g, s][:],
+                in_=response[PASS * g : PASS * (g + 1), PASS * s : PASS * (s + 1)].rearrange("(p j) b -> p j b", j=PACK),
+            )
+
+        ident = keep.tile([P, P], F32, name="ident")
+        vec_raw = keep.tile([P, 2 * P], BF16, name="vec_raw")
+        site_plane_raw = keep.tile([P, B], U8, name="site_plane_raw", align_bytes=64)
+        plant_plane = keep.tile([P, NP], U8, name="plant_plane", align_bytes=64)
+        site_raw = keep.tile([P, 2 * B], U8, name="site_raw", align_bytes=64)
+        plant = keep.tile([P, 2 * NP], U8, name="plant", align_bytes=64)
+        warm = keep.tile([P, 1], F32, name="warm")
+
+        nc.gpsimd.memset(plant_plane[:].bitcast(I32), 0)
+        nc.vector.memset(site_plane_raw[:].bitcast(I32), 0)
+        nc.vector.memset(vec_raw[:], 0.0)
+
+        def load_scale_rows(queue, plane, scales):
+            for r in range(4):
+                queue.dma_start(out=plane[r:P:32, :].bitcast(I32), in_=scales[0, r:16:4, :].bitcast(I32))
+
+        load_response(0, 0)
+        nc.sync.dma_start(out=site_raw[:].bitcast(I32), in_=site_words[0].bitcast(I32))
+        load_scale_rows(nc.sync, site_plane_raw, site_scales)
+        nc.sync.dma_start(out=plant[:].bitcast(I32), in_=plant_words[0].bitcast(I32))
+        load_response(1, 0)
+        load_scale_rows(nc.gpsimd, plant_plane, plant_scales)
+        make_identity(nc, ident[:])
+        nc.scalar.activation(out=warm[:], in_=vec_raw[:, 2 * P - 1 : 2 * P], func=ACT.Relu)
+        for row, vec in ((0, base), (PACK, cap)):
+            nc.gpsimd.dma_start(
+                out=vec_raw[row : row + PACK, :].rearrange("t (m r) -> t m r", r=4),
+                in_=vec.rearrange("(m t r) -> t m r", t=PACK, r=4),
+            )
+        load_weather(0)
+        load_weather(1)
+        load_response(0, 1)
+        load_response(1, 1)
+        for h in range(2, 2 * CHUNKS):
+            load_weather(h)
+
+        w_grouped, w_mx, r_grouped, r_mx = {}, {}, {}, {}
+        l_slots, l_grouped, l_mx = {}, {}, {}
+        c_slots, c_grouped, c_mx = {}, {}, {}
+        banks = {}
+        vec = keep.tile([P, 2, 2 * PACK], F32, name="vec")
+        vec_f32 = keep.tile([P, 2 * P], F32, name="vec_f32")
+        site = keep.tile([P, 2 * B], U8, name="site", align_bytes=64)
+        site_plane = keep.tile([P, B], U8, name="site_plane", align_bytes=64)
+
+        def turn_weather(h, g, engine):
+            c, hh = divmod(h, 2)
+            if hh == 0:
+                w_grouped[c, g] = work.tile([P, PACK * CHUNK], BF16, name="w_grouped", bufs=4, align_bytes=64)
+            bank = take_bank("turn")
+            words = w_raw[h][:].bitcast(F32)
+            for e in range(2):
+                for u in range(2):
+                    col = P * (2 * e + u)
+                    nc.tensor.transpose(bank[:, col : col + P], words[:, e, HALF * g + u : HALF * (g + 1) : 2], ident[:])
+            copy_on(
+                engine,
+                w_grouped[c, g][:].bitcast(F32)[:, CHUNK * hh : CHUNK * (hh + 1)].rearrange("p (e n u) -> p e n u", e=2, u=2),
+                bank[:].rearrange("p (e u n) -> p e n u", e=2, u=2),
+            )
+            give_bank("turn")
+
+        def quantize_weather(c, g):
+            w_mx[c, g] = mx_tiles("w%d%d" % (c, g))
+            quantize(w_mx[c, g], w_grouped[c, g])
+
+        def group_response(g, s, engine):
+            r_grouped[g, s] = grouped_tile("r_grouped")
+            copy_on(
+                engine,
+                r_grouped[g, s][:].rearrange("p (t m r j) -> p t m j r", t=PACK, r=4, j=PACK),
+                r_raw[g, s][:].rearrange("p j (m t r) -> p t m j r", t=PACK, r=4),
+            )
+
+        def quantize_response(g, s):
+            r_mx[g, s] = mx_tiles("r%d%d" % (g, s))
+            quantize(r_mx[g, s], r_grouped[g, s])
+
+        def widen_vectors():
+            nc.vector.tensor_copy(out=vec_f32[:], in_=vec_raw[:])
+
+        def turn_vectors():
+            bank = take_bank("vec")
+            for s in range(2):
+                nc.tensor.transpose(bank[:, P * s : P * (s + 1)], vec_f32[:, P * s : P * (s + 1)], ident[:])
+            nc.scalar.copy(out=vec[:], in_=bank[:, 0 : 2 * P].rearrange("p (s n) -> p s n", s=2)[:, :, 0 : 2 * PACK])
+            give_bank("vec")
+
+        def order_site():
+            nc.vector.tensor_copy(
+                out=site[:].bitcast(I32).rearrange("p (s t m w) -> p s t m w", s=2, t=PACK, w=2),
+                in_=site_raw[:].bitcast(I32).rearrange("p (s m t w) -> p s t m w", s=2, t=PACK, w=2),
+            )
+            nc.vector.tensor_copy(
+                out=site_plane[:].bitcast(I32).rearrange("p (s t m) -> p s t m", s=2, t=PACK),
+                in_=site_plane_raw[:].bitcast(I32).rearrange("p (s m t) -> p s t m", s=2, t=PACK),
+            )
+
+        def mx_pass(acc, stationary, j, moving, cols, start, stop):
+            own = slice(P * j, P * (j + 1))
+            nc.tensor.matmul_mx(
+                out=acc,
+                lhsT=stationary[0][:, own].bitcast(FP8X4),
+                lhsT_scale=stationary[1][:, own],
+                rhs=moving[0][:, cols].bitcast(FP8X4),
+                rhs_scale=moving[1][:, cols],
+                start=start,
+                stop=stop,
+            )
+
+        def load_pass(c, s, t, g, cols=ALL):
+            if g == 0:
+                banks["l", t] = take_bank(("l", t))
+            mx_pass(banks["l", t][:, cols], r_mx[g, s], t, w_mx[c, g], cols, g == 0, g == 1)
+
+        def relu_out(c, s, t, engine, cols=ALL):
+            if (c, s) not in l_slots:
+                l_slots[c, s] = work.tile([P, PACK, CHUNK], BF16, name="l_slots", tag="slots", bufs=6)
+            bias = vec[:, s, t : t + 1]
+            row = l_slots[c, s][:, t, cols]
+            if engine == "scalar":
+                nc.scalar.activation(out=row, in_=banks["l", t][:, cols], func=ACT.Relu, bias=bias)
+            else:
+                nc.vector.tensor_scalar(
+                    out=row, in0=banks["l", t][:, cols], scalar1=bias, scalar2=0.0, op0=ALU.add, op1=ALU.max
+                )
+            give_bank(("l", t))
+
+        def loads(c, s, t, engine="scalar", cols=ALL):
+            for g in range(2):
+                load_pass(c, s, t, g, cols)
+            relu_out(c, s, t, engine, cols)
+
+        def clip(c, s, t, cols=ALL):
+            row = l_slots[c, s][:, t, cols]
+            nc.vector.tensor_scalar(
+                out=row, in0=row, scalar1=vec[:, s, PACK + t : PACK + t + 1], scalar2=None, op0=ALU.min
+            )
+
+        def group_load(c, s, cols=ALL):
+            if (c, s) not in l_grouped:
+                l_grouped[c, s] = grouped_tile("l_grouped")
+            interleave("vector", l_grouped[c, s], l_slots[c, s], cols)
+
+        def quantize_load(c, s, cols=ALL):
+            if (c, s) not in l_mx:
+                l_mx[c, s] = mx_tiles("l%d%d" % (c, s))
+            quantize(l_mx[c, s], l_grouped[c, s], cols)
+
+        def coefficient_pass(s, t):
+            i = PACK * s + t
+            banks["c", i] = take_bank(("c", i))
+            nc.tensor.matmul_mx(
+                out=banks["c", i][:],
+                lhsT=site[:, 2 * P * i : 2 * P * (i + 1)].bitcast(FP4X4),
+                lhsT_scale=site_plane[:, P * i : P * (i + 1)],
+                rhs=plant[:].bitcast(FP4X4),
+                rhs_scale=plant_plane[:],
+                start=True,
+                stop=True,
+            )
+
+        def coefficient_out(s, t, engine):
+            if t == 0:
+                c_slots[s] = work.tile([P, PACK, NP], BF16, name="c_slots", tag="slots", bufs=6)
+            copy_on(engine, c_slots[s][:, t, :], banks["c", PACK * s + t][:])
+            give_bank(("c", PACK * s + t))
+
+        def group_coefficients(s):
+            c_grouped[s] = grouped_tile("c_grouped")
+            interleave("vector", c_grouped[s], c_slots[s])
+
+        def quantize_coefficients(s):
+            c_mx[s] = mx_tiles("c%d" % s)
+            quantize(c_mx[s], c_grouped[s])
+
+        def plant_pass(c, j, s):
+            if s == 0:
+                banks["o", j] = take_bank(("o", j))
+            mx_pass(banks["o", j][:], l_mx[c, s], j, c_mx[s], ALL, s == 0, s == 1)
+
+        def store(c, j, engine):
+            hh, e = divmod(j, 2)
+            result = work.tile([P, NP], F32, name="result", bufs=6)
+            copy_on(engine, result[:], banks["o", j][:])
+            give_bank(("o", j))
+            rows = out[CHUNK * c + HALF * hh : CHUNK * c + HALF * (hh + 1), :].rearrange("(n e) q -> n e q", e=2)
+            nc.sync.dma_start(out=rows[:, e, :], in_=result[:])
+
+        def plants(c, j, engine):
+            for s in range(2):
+                plant_pass(c, j, s)
+            store(c, j, engine)
+
+        group_response(0, 0, "vector")
+        order_site()
+        quantize_response(0, 0)
+        group_response(1, 0, "vector")
+        for t in range(PACK):
+            coefficient_pass(0, t)
+            coefficient_out(0, t, "scalar")
+        widen_vectors()
+        quantize_response(1, 0)
+        for h in range(2):
+            for g in range(2):
+                turn_weather(h, g, "scalar")
+            if h == 1:
+                turn_vectors()
+            for t in (2 * h, 2 * h + 1):
+                coefficient_pass(1, t)
+        for t in range(PACK):
+            coefficient_out(1, t, "scalar")
+        group_coefficients(0)
+        group_response(0, 1, "vector")
+        quantize_weather(0, 0)
+        quantize_weather(0, 1)
+        group_response(1, 1, "vector")
+        quantize_response(0, 1)
+        quantize_response(1, 1)
+
+        last = CHUNKS - 1
+        for c in range(last):
+            if c == 0:
+                for g in range(2):
+                    for t in range(PACK):
+                        load_pass(c, 0, t, g)
+                for t in range(PACK):
+                    relu_out(c, 0, t, "scalar")
+            else:
+                for t in range(PACK):
+                    loads(c, 0, t)
+            if c > 0:
+                group_load(c - 1, 1)
+            if c == 1:
+                group_coefficients(1)
+            if c > 0:
+                quantize_load(c - 1, 1)
+            if c == 1:
+                quantize_coefficients(1)
+            for t in range(PACK):
+                clip(c, 0, t)
+            for hh in range(2):
+                turn_weather(2 * c + 2 + hh, 0, "scalar")
+            loads(c, 1, 0)
+            for hh in range(2):
+                turn_weather(2 * c + 2 + hh, 1, "scalar")
+            quantize_weather(c + 1, 0)
+            group_load(c, 0)
+            quantize_weather(c + 1, 1)
+            quantize_load(c, 0)
+            if c == 0:
+                quantize_coefficients(0)
+            for t in range(1, PACK):
+                loads(c, 1, t)
+            for t in range(PACK):
+                clip(c, 1, t)
+            if c > 0:
+                for j in range(4):
+                    plants(c - 1, j, "vector" if j == 3 or (c == 2 and j == 2) else "scalar")
+        c = last
+        for t in range(PACK):
+            loads(c, 0, t)
+        group_load(c - 1, 1)
+        clip(c, 0, 0)
+        quantize_load(c - 1, 1)
+        for t in range(1, PACK):
+            clip(c, 0, t)
+        group_load(c, 0)
+        for t in range(PACK):
+            loads(c, 1, t, cols=HALVES[0])
+        clip(c, 1, 0, HALVES[0])
+        quantize_load(c, 0)
+        for t in range(1, PACK):
+            clip(c, 1, t, HALVES[0])
+        for j in range(2):
+            plants(c - 1, j, "scalar")
+        group_load(c, 1, HALVES[0])
+        for t in range(PACK):
+            loads(c, 1, t, cols=HALVES[1])
+        clip(c, 1, 0, HALVES[1])
+        quantize_load(c, 1, HALVES[0])
+        for t in range(1, PACK):
+            clip(c, 1, t, HALVES[1])
+        group_load(c, 1, HALVES[1])
+        quantize_load(c, 1, HALVES[1])
+        for j in range(2, 4):
+            plants(c - 1, j, "scalar")
+        for j in range(2):
+            plants(c, j, "scalar")
+        for s in range(2):
+            for j in range(2, 4):
+                plant_pass(c, j, s)
+        store(c, 2, "vector")
+        store(c, 3, "scalar")

@@ -98,29 +98,34 @@ def tile_district_heat_dispatch_s12_kernel(
         plant = keep.tile([P, 2 * NP], U8, name="plant", align_bytes=64)
         warm = keep.tile([P, 1], F32, name="warm")
 
-        nc.gpsimd.memset(plant_plane[:].bitcast(I32), 0)
         nc.vector.memset(site_plane_raw[:].bitcast(I32), 0)
+        nc.vector.memset(plant_plane[:].bitcast(I32), 0)
         nc.vector.memset(vec_raw[:], 0.0)
+        nc.vector.memset(warm[:], 0.0)
+        make_identity(nc, ident[:])
+        nc.scalar.activation(out=warm[:], in_=warm[:], func=ACT.Relu)
 
-        def load_scale_rows(queue, plane, scales):
-            for r in range(4):
-                queue.dma_start(out=plane[r:P:32, :].bitcast(I32), in_=scales[0, r:16:4, :].bitcast(I32))
+        def load_scale_row(plane, scales, r):
+            nc.sync.dma_start(out=plane[r:P:32, :].bitcast(I32), in_=scales[0, r:16:4, :].bitcast(I32))
+
+        def load_vector(row, vector):
+            nc.sync.dma_start(
+                out=vec_raw[row : row + PACK, :].rearrange("t (m r) -> t m r", r=4),
+                in_=vector.rearrange("(m t r) -> t m r", t=PACK, r=4),
+            )
 
         load_response(0, 0)
+        for r in range(4):
+            load_scale_row(site_plane_raw, site_scales, r)
         nc.sync.dma_start(out=site_raw[:].bitcast(I32), in_=site_words[0].bitcast(I32))
-        load_scale_rows(nc.sync, site_plane_raw, site_scales)
         nc.sync.dma_start(out=plant[:].bitcast(I32), in_=plant_words[0].bitcast(I32))
-        load_response(1, 0)
-        load_scale_rows(nc.gpsimd, plant_plane, plant_scales)
-        make_identity(nc, ident[:])
-        nc.scalar.activation(out=warm[:], in_=vec_raw[:, 2 * P - 1 : 2 * P], func=ACT.Relu)
-        for row, vec in ((0, base), (PACK, cap)):
-            nc.gpsimd.dma_start(
-                out=vec_raw[row : row + PACK, :].rearrange("t (m r) -> t m r", r=4),
-                in_=vec.rearrange("(m t r) -> t m r", t=PACK, r=4),
-            )
+        for r in range(4):
+            load_scale_row(plant_plane, plant_scales, r)
         load_weather(0)
+        load_response(1, 0)
         load_weather(1)
+        load_vector(0, base)
+        load_vector(PACK, cap)
         load_response(0, 1)
         load_response(1, 1)
         for h in range(2, 2 * CHUNKS):
@@ -287,25 +292,27 @@ def tile_district_heat_dispatch_s12_kernel(
         group_response(0, 0, "vector")
         order_site()
         quantize_response(0, 0)
-        group_response(1, 0, "vector")
         for t in range(PACK):
             coefficient_pass(0, t)
-            coefficient_out(0, t, "scalar")
+            coefficient_out(0, t, "scalar" if t % 2 else "vector")
+        for g in range(2):
+            turn_weather(0, g, "scalar")
+        group_response(1, 0, "vector")
+        for t in range(2):
+            coefficient_pass(1, t)
+        coefficient_out(1, 0, "scalar")
         widen_vectors()
         quantize_response(1, 0)
-        for h in range(2):
-            for g in range(2):
-                turn_weather(h, g, "scalar")
-            if h == 1:
-                turn_vectors()
-            for t in (2 * h, 2 * h + 1):
-                coefficient_pass(1, t)
-        for t in range(PACK):
+        for g in range(2):
+            turn_weather(1, g, "scalar")
+        turn_vectors()
+        for t in range(2, PACK):
+            coefficient_pass(1, t)
+        for t in range(1, PACK):
             coefficient_out(1, t, "scalar")
-        group_coefficients(0)
-        group_response(0, 1, "vector")
         quantize_weather(0, 0)
         quantize_weather(0, 1)
+        group_response(0, 1, "vector")
         group_response(1, 1, "vector")
         quantize_response(0, 1)
         quantize_response(1, 1)
@@ -324,24 +331,30 @@ def tile_district_heat_dispatch_s12_kernel(
             if c > 0:
                 group_load(c - 1, 1)
             if c == 1:
-                group_coefficients(1)
+                quantize_coefficients(1)
             if c > 0:
                 quantize_load(c - 1, 1)
-            if c == 1:
-                quantize_coefficients(1)
             for t in range(PACK):
                 clip(c, 0, t)
             for hh in range(2):
                 turn_weather(2 * c + 2 + hh, 0, "scalar")
-            loads(c, 1, 0)
+            if c > 0:
+                loads(c, 1, 0)
             for hh in range(2):
                 turn_weather(2 * c + 2 + hh, 1, "scalar")
-            quantize_weather(c + 1, 0)
-            group_load(c, 0)
-            quantize_weather(c + 1, 1)
-            quantize_load(c, 0)
             if c == 0:
+                loads(c, 1, 0)
+            if c == 0:
+                group_coefficients(0)
+            quantize_weather(c + 1, 0)
+            if c > 0:
+                group_load(c, 0)
+            quantize_weather(c + 1, 1)
+            if c == 0:
+                group_load(c, 0)
                 quantize_coefficients(0)
+                group_coefficients(1)
+            quantize_load(c, 0)
             for t in range(1, PACK):
                 loads(c, 1, t)
             for t in range(PACK):

@@ -91,7 +91,7 @@ def tile_district_heat_dispatch_s12_kernel(
             )
 
         ident = keep.tile([P, P], F32, name="ident")
-        vec_raw = keep.tile([P, 2 * P], BF16, name="vec_raw")
+        vec_raw = keep.tile([P, PASS], BF16, name="vec_raw")
         site_plane_raw = keep.tile([P, B], U8, name="site_plane_raw", align_bytes=64)
         plant_plane = keep.tile([P, NP], U8, name="plant_plane", align_bytes=64)
         site_raw = keep.tile([P, 2 * B], U8, name="site_raw", align_bytes=64)
@@ -109,23 +109,20 @@ def tile_district_heat_dispatch_s12_kernel(
             nc.sync.dma_start(out=plane[r:P:32, :].bitcast(I32), in_=scales[0, r:16:4, :].bitcast(I32))
 
         def load_vector(row, vector):
-            nc.sync.dma_start(
-                out=vec_raw[row : row + PACK, :].rearrange("t (m r) -> t m r", r=4),
-                in_=vector.rearrange("(m t r) -> t m r", t=PACK, r=4),
-            )
+            nc.sync.dma_start(out=vec_raw[row : row + 2, :], in_=vector.rearrange("(s b) -> s b", s=2))
 
         load_response(0, 0)
         for r in range(4):
             load_scale_row(site_plane_raw, site_scales, r)
         nc.sync.dma_start(out=site_raw[:].bitcast(I32), in_=site_words[0].bitcast(I32))
+        load_response(1, 0)
         nc.sync.dma_start(out=plant[:].bitcast(I32), in_=plant_words[0].bitcast(I32))
         for r in range(4):
             load_scale_row(plant_plane, plant_scales, r)
         load_weather(0)
-        load_response(1, 0)
         load_weather(1)
         load_vector(0, base)
-        load_vector(PACK, cap)
+        load_vector(2, cap)
         load_response(0, 1)
         load_response(1, 1)
         for h in range(2, 2 * CHUNKS):
@@ -135,8 +132,8 @@ def tile_district_heat_dispatch_s12_kernel(
         l_slots, l_grouped, l_mx = {}, {}, {}
         c_slots, c_grouped, c_mx = {}, {}, {}
         banks = {}
-        vec = keep.tile([P, 2, 2 * PACK], F32, name="vec")
-        vec_f32 = keep.tile([P, 2 * P], F32, name="vec_f32")
+        vec = keep.tile([P, PACK, 4], F32, name="vec")
+        vec_f32 = keep.tile([P, PASS], F32, name="vec_f32")
         site = keep.tile([P, 2 * B], U8, name="site", align_bytes=64)
         site_plane = keep.tile([P, B], U8, name="site_plane", align_bytes=64)
 
@@ -157,9 +154,10 @@ def tile_district_heat_dispatch_s12_kernel(
             )
             give_bank("turn")
 
-        def quantize_weather(c, g):
-            w_mx[c, g] = mx_tiles("w%d%d" % (c, g))
-            quantize(w_mx[c, g], w_grouped[c, g])
+        def quantize_weather(c, g, cols=ALL):
+            if (c, g) not in w_mx:
+                w_mx[c, g] = mx_tiles("w%d%d" % (c, g))
+            quantize(w_mx[c, g], w_grouped[c, g], cols)
 
         def group_response(g, s, engine):
             r_grouped[g, s] = grouped_tile("r_grouped")
@@ -174,13 +172,16 @@ def tile_district_heat_dispatch_s12_kernel(
             quantize(r_mx[g, s], r_grouped[g, s])
 
         def widen_vectors():
-            nc.vector.tensor_copy(out=vec_f32[:], in_=vec_raw[:])
+            nc.vector.tensor_copy(
+                out=vec_f32[:].rearrange("p (t m r) -> p t m r", t=PACK, r=4),
+                in_=vec_raw[:].rearrange("p (m t r) -> p t m r", t=PACK, r=4),
+            )
 
         def turn_vectors():
             bank = take_bank("vec")
-            for s in range(2):
-                nc.tensor.transpose(bank[:, P * s : P * (s + 1)], vec_f32[:, P * s : P * (s + 1)], ident[:])
-            nc.scalar.copy(out=vec[:], in_=bank[:, 0 : 2 * P].rearrange("p (s n) -> p s n", s=2)[:, :, 0 : 2 * PACK])
+            for t in range(PACK):
+                nc.tensor.transpose(bank[:, P * t : P * (t + 1)], vec_f32[:, P * t : P * (t + 1)], ident[:])
+            nc.scalar.copy(out=vec[:], in_=bank[:].rearrange("p (t n) -> p t n", t=PACK)[:, :, 0:4])
             give_bank("vec")
 
         def order_site():
@@ -205,15 +206,15 @@ def tile_district_heat_dispatch_s12_kernel(
                 stop=stop,
             )
 
-        def load_pass(c, s, t, g, cols=ALL):
-            if g == 0:
+        def load_pass(c, s, t, g, cols=ALL, new_bank=True):
+            if g == 0 and new_bank:
                 banks["l", t] = take_bank(("l", t))
             mx_pass(banks["l", t][:, cols], r_mx[g, s], t, w_mx[c, g], cols, g == 0, g == 1)
 
         def relu_out(c, s, t, engine, cols=ALL):
             if (c, s) not in l_slots:
                 l_slots[c, s] = work.tile([P, PACK, CHUNK], BF16, name="l_slots", tag="slots", bufs=6)
-            bias = vec[:, s, t : t + 1]
+            bias = vec[:, t, s : s + 1]
             row = l_slots[c, s][:, t, cols]
             if engine == "scalar":
                 nc.scalar.activation(out=row, in_=banks["l", t][:, cols], func=ACT.Relu, bias=bias)
@@ -231,7 +232,7 @@ def tile_district_heat_dispatch_s12_kernel(
         def clip(c, s, t, cols=ALL):
             row = l_slots[c, s][:, t, cols]
             nc.vector.tensor_scalar(
-                out=row, in0=row, scalar1=vec[:, s, PACK + t : PACK + t + 1], scalar2=None, op0=ALU.min
+                out=row, in0=row, scalar1=vec[:, t, 2 + s : 3 + s], scalar2=None, op0=ALU.min
             )
 
         def group_load(c, s, cols=ALL):
@@ -278,7 +279,7 @@ def tile_district_heat_dispatch_s12_kernel(
 
         def store(c, j, engine):
             hh, e = divmod(j, 2)
-            result = work.tile([P, NP], F32, name="result", bufs=6)
+            result = work.tile([P, NP], F32, name="result", bufs=8)
             copy_on(engine, result[:], banks["o", j][:])
             give_bank(("o", j))
             rows = out[CHUNK * c + HALF * hh : CHUNK * c + HALF * (hh + 1), :].rearrange("(n e) q -> n e q", e=2)
@@ -289,105 +290,114 @@ def tile_district_heat_dispatch_s12_kernel(
                 plant_pass(c, j, s)
             store(c, j, engine)
 
+        def turn_pass(c, g, second="scalar"):
+            turn_weather(2 * c, g, "scalar")
+            turn_weather(2 * c + 1, g, second)
+
         group_response(0, 0, "vector")
         order_site()
         quantize_response(0, 0)
+        group_response(1, 0, "vector")
         for t in range(PACK):
             coefficient_pass(0, t)
-            coefficient_out(0, t, "scalar" if t % 2 else "vector")
-        for g in range(2):
-            turn_weather(0, g, "scalar")
-        group_response(1, 0, "vector")
-        for t in range(2):
-            coefficient_pass(1, t)
-        coefficient_out(1, 0, "scalar")
-        widen_vectors()
+            coefficient_out(0, t, "vector" if t == 1 else "scalar")
         quantize_response(1, 0)
-        for g in range(2):
-            turn_weather(1, g, "scalar")
+        turn_pass(0, 0)
+        widen_vectors()
+        for t in range(PACK):
+            coefficient_pass(1, t)
+        coefficient_out(1, 0, "vector")
+        coefficient_out(1, 1, "scalar")
+        turn_pass(0, 1)
+        quantize_weather(0, 0)
+        group_response(0, 1, "vector")
         turn_vectors()
         for t in range(2, PACK):
-            coefficient_pass(1, t)
-        for t in range(1, PACK):
             coefficient_out(1, t, "scalar")
-        quantize_weather(0, 0)
+        for t in range(PACK):
+            load_pass(0, 0, t, 0)
         quantize_weather(0, 1)
-        group_response(0, 1, "vector")
         group_response(1, 1, "vector")
         quantize_response(0, 1)
         quantize_response(1, 1)
 
+        def load_group(c, s, ts, cols=ALL):
+            for t in ts:
+                loads(c, s, t, cols=cols)
+
+        def clips(c, s, ts, cols=ALL):
+            for t in ts:
+                clip(c, s, t, cols)
+
+        group_coefficients(0)
+        for t in range(PACK):
+            load_pass(0, 0, t, 1)
+            relu_out(0, 0, t, "scalar")
+        turn_pass(1, 0)
+        for t in range(PACK):
+            load_pass(0, 1, t, 0)
+        turn_pass(1, 1)
+        for t in range(PACK):
+            load_pass(0, 1, t, 1)
+            relu_out(0, 1, t, "scalar")
+        clips(0, 0, range(PACK))
+        quantize_weather(1, 0)
+        group_coefficients(1)
+        quantize_weather(1, 1)
+        group_load(0, 0)
+        quantize_coefficients(0)
+        clips(0, 1, range(PACK))
+        quantize_load(0, 0)
+        group_load(0, 1)
+        quantize_coefficients(1)
+        quantize_load(0, 1)
+
         last = CHUNKS - 1
-        for c in range(last):
-            if c == 0:
-                for g in range(2):
-                    for t in range(PACK):
-                        load_pass(c, 0, t, g)
-                for t in range(PACK):
-                    relu_out(c, 0, t, "scalar")
-            else:
-                for t in range(PACK):
-                    loads(c, 0, t)
-            if c > 0:
-                group_load(c - 1, 1)
-            if c == 1:
-                quantize_coefficients(1)
-            if c > 0:
+        for c in range(1, last):
+            turn_pass(c + 1, 0, "vector" if c == 2 else "scalar")
+            if c == 2:
                 quantize_load(c - 1, 1)
-            for t in range(PACK):
-                clip(c, 0, t)
-            for hh in range(2):
-                turn_weather(2 * c + 2 + hh, 0, "scalar")
-            if c > 0:
-                loads(c, 1, 0)
-            for hh in range(2):
-                turn_weather(2 * c + 2 + hh, 1, "scalar")
-            if c == 0:
-                loads(c, 1, 0)
-            if c == 0:
-                group_coefficients(0)
-            quantize_weather(c + 1, 0)
-            if c > 0:
-                group_load(c, 0)
+            load_group(c, 0, range(PACK))
+            if c == 2:
+                quantize_weather(c + 1, 0)
+            clips(c, 0, range(PACK))
+            turn_pass(c + 1, 1, "vector" if c == 2 else "scalar")
+            load_group(c, 1, range(PACK))
+            if c == 1:
+                quantize_weather(c + 1, 0)
+            group_load(c, 0)
             quantize_weather(c + 1, 1)
-            if c == 0:
-                group_load(c, 0)
-                quantize_coefficients(0)
-                group_coefficients(1)
             quantize_load(c, 0)
-            for t in range(1, PACK):
-                loads(c, 1, t)
-            for t in range(PACK):
-                clip(c, 1, t)
-            if c > 0:
-                for j in range(4):
-                    plants(c - 1, j, "vector" if j == 3 or (c == 2 and j == 2) else "scalar")
+            clips(c, 1, range(PACK))
+            for j in range(4):
+                for s in range(2):
+                    plant_pass(c - 1, j, s)
+            for j in range(3):
+                store(c - 1, j, "scalar")
+            group_load(c, 1)
+            if c == 2:
+                store(c - 1, 3, "vector")
+                quantize_load(c, 1)
+            else:
+                store(c - 1, 3, "scalar")
         c = last
-        for t in range(PACK):
-            loads(c, 0, t)
-        group_load(c - 1, 1)
-        clip(c, 0, 0)
-        quantize_load(c - 1, 1)
-        for t in range(1, PACK):
-            clip(c, 0, t)
+        load_group(c, 0, range(PACK))
+        clips(c, 0, range(PACK))
         group_load(c, 0)
-        for t in range(PACK):
-            loads(c, 1, t, cols=HALVES[0])
-        clip(c, 1, 0, HALVES[0])
+        load_group(c, 1, range(PACK), HALVES[0])
+        clips(c, 1, range(PACK), HALVES[0])
         quantize_load(c, 0)
-        for t in range(1, PACK):
-            clip(c, 1, t, HALVES[0])
-        for j in range(2):
-            plants(c - 1, j, "scalar")
         group_load(c, 1, HALVES[0])
-        for t in range(PACK):
-            loads(c, 1, t, cols=HALVES[1])
-        clip(c, 1, 0, HALVES[1])
+        for j in range(2):
+            for s in range(2):
+                plant_pass(c - 1, j, s)
+        store(c - 1, 0, "scalar")
+        load_group(c, 1, range(PACK), HALVES[1])
+        clips(c, 1, range(PACK), HALVES[1])
         quantize_load(c, 1, HALVES[0])
-        for t in range(1, PACK):
-            clip(c, 1, t, HALVES[1])
         group_load(c, 1, HALVES[1])
         quantize_load(c, 1, HALVES[1])
+        store(c - 1, 1, "scalar")
         for j in range(2, 4):
             plants(c - 1, j, "scalar")
         for j in range(2):

@@ -111,15 +111,15 @@ def tile_district_heat_dispatch_s12_kernel(
         def load_vector(row, vector):
             nc.sync.dma_start(out=vec_raw[row : row + 2, :], in_=vector.rearrange("(s b) -> s b", s=2))
 
-        load_response(0, 0)
+        load_weather(0)
         for r in range(4):
             load_scale_row(site_plane_raw, site_scales, r)
         nc.sync.dma_start(out=site_raw[:].bitcast(I32), in_=site_words[0].bitcast(I32))
-        load_response(1, 0)
+        load_response(0, 0)
         nc.sync.dma_start(out=plant[:].bitcast(I32), in_=plant_words[0].bitcast(I32))
         for r in range(4):
             load_scale_row(plant_plane, plant_scales, r)
-        load_weather(0)
+        load_response(1, 0)
         load_weather(1)
         load_vector(0, base)
         load_vector(2, cap)
@@ -294,29 +294,35 @@ def tile_district_heat_dispatch_s12_kernel(
             turn_weather(2 * c, g, "scalar")
             turn_weather(2 * c + 1, g, second)
 
-        group_response(0, 0, "vector")
+        for g in range(2):
+            turn_weather(0, g, "scalar")
         order_site()
-        quantize_response(0, 0)
-        group_response(1, 0, "vector")
+        quantize_weather(0, 0, HALVES[0])
+        group_response(0, 0, "vector")
+        quantize_weather(0, 1, HALVES[0])
         for t in range(PACK):
             coefficient_pass(0, t)
-            coefficient_out(0, t, "vector" if t == 1 else "scalar")
-        quantize_response(1, 0)
-        turn_pass(0, 0)
-        widen_vectors()
-        for t in range(PACK):
+        for t in range(2):
             coefficient_pass(1, t)
+        quantize_response(0, 0)
+        group_response(1, 0, "vector")
+        quantize_response(1, 0)
+        for t in range(PACK):
+            coefficient_out(0, t, "scalar")
         coefficient_out(1, 0, "vector")
-        coefficient_out(1, 1, "scalar")
-        turn_pass(0, 1)
-        quantize_weather(0, 0)
+        widen_vectors()
+        for g in range(2):
+            turn_weather(1, g, "scalar")
+        quantize_weather(0, 0, HALVES[1])
+        quantize_weather(0, 1, HALVES[1])
         group_response(0, 1, "vector")
-        turn_vectors()
         for t in range(2, PACK):
+            coefficient_pass(1, t)
+        turn_vectors()
+        for t in range(1, PACK):
             coefficient_out(1, t, "scalar")
         for t in range(PACK):
             load_pass(0, 0, t, 0)
-        quantize_weather(0, 1)
         group_response(1, 1, "vector")
         quantize_response(0, 1)
         quantize_response(1, 1)
@@ -356,12 +362,12 @@ def tile_district_heat_dispatch_s12_kernel(
         for c in range(1, last):
             turn_pass(c + 1, 0, "vector" if c == 2 else "scalar")
             if c == 2:
+                group_load(c - 1, 1)
+                quantize_weather(c + 1, 0)
                 quantize_load(c - 1, 1)
             load_group(c, 0, range(PACK))
-            if c == 2:
-                quantize_weather(c + 1, 0)
             clips(c, 0, range(PACK))
-            turn_pass(c + 1, 1, "vector" if c == 2 else "scalar")
+            turn_pass(c + 1, 1)
             load_group(c, 1, range(PACK))
             if c == 1:
                 quantize_weather(c + 1, 0)
@@ -369,35 +375,29 @@ def tile_district_heat_dispatch_s12_kernel(
             quantize_weather(c + 1, 1)
             quantize_load(c, 0)
             clips(c, 1, range(PACK))
-            for j in range(4):
-                for s in range(2):
-                    plant_pass(c - 1, j, s)
-            for j in range(3):
-                store(c - 1, j, "scalar")
-            group_load(c, 1)
             if c == 2:
-                store(c - 1, 3, "vector")
+                load_group(last, 0, range(PACK))
+                group_load(c, 1)
+                clips(last, 0, range(PACK))
                 quantize_load(c, 1)
-            else:
-                store(c - 1, 3, "scalar")
+                group_load(last, 0)
+            for j in range(4):
+                plants(c - 1, j, "vector" if c == 2 and j == 3 else "scalar")
         c = last
-        load_group(c, 0, range(PACK))
-        clips(c, 0, range(PACK))
-        group_load(c, 0)
+        quantize_load(c, 0)
         load_group(c, 1, range(PACK), HALVES[0])
         clips(c, 1, range(PACK), HALVES[0])
-        quantize_load(c, 0)
         group_load(c, 1, HALVES[0])
         for j in range(2):
             for s in range(2):
                 plant_pass(c - 1, j, s)
         store(c - 1, 0, "scalar")
+        store(c - 1, 1, "vector")
         load_group(c, 1, range(PACK), HALVES[1])
         clips(c, 1, range(PACK), HALVES[1])
         quantize_load(c, 1, HALVES[0])
         group_load(c, 1, HALVES[1])
         quantize_load(c, 1, HALVES[1])
-        store(c - 1, 1, "scalar")
         for j in range(2, 4):
             plants(c - 1, j, "scalar")
         for j in range(2):

@@ -3,8 +3,8 @@ from contextlib import ExitStack
 import concourse.mybir as mybir
 from concourse.masks import make_identity
 
-T, K, B, A, NP = 2048, 1024, 1024, 512, 512
-FLOPS = 2 * T * K * B + 2 * A * B * NP + 2 * T * B * NP
+T, K, B, A, PLANTS = 2048, 1024, 1024, 512, 512
+FLOPS = 2 * T * K * B + 2 * A * B * PLANTS + 2 * T * B * PLANTS
 
 F32 = mybir.dt.float32
 BF16 = mybir.dt.bfloat16
@@ -17,14 +17,21 @@ ALU = mybir.AluOpType
 ACT = mybir.ActivationFunctionType
 
 P = 128
-PACK = 4
-PASS = P * PACK
-CHUNK = 512
-HALF = 256
-CHUNKS = T // CHUNK
+SLOTS = 4
+PASS = P * SLOTS
+RUN = 4
+WIDTH = 512
+HALF = WIDTH // 2
 BANKS = 8
-ALL = slice(0, CHUNK)
-HALVES = (slice(0, HALF), slice(HALF, CHUNK))
+ALL = slice(0, WIDTH)
+FIRST, SECOND = slice(0, HALF), slice(HALF, WIDTH)
+SCALE_ROWS = 16
+QUADRANT = 32
+
+TURNED_BUFS = 4
+GROUPED_BUFS = 4
+SLOT_BUFS = 6
+RESULT_BUFS = 8
 
 
 def tile_district_heat_dispatch_s12_kernel(
@@ -33,19 +40,20 @@ def tile_district_heat_dispatch_s12_kernel(
     nc = tc.nc
     with ExitStack() as ctx:
         keep = ctx.enter_context(tc.tile_pool(name="keep", bufs=1))
-        work = ctx.enter_context(tc.tile_pool(name="work", bufs=3))
+        work = ctx.enter_context(tc.tile_pool(name="work", bufs=1))
         psum = ctx.enter_context(tc.psum_pool(name="psum", bufs=1))
         ctx.enter_context(tc.manual_schedule())
 
         free_banks = list(range(BANKS))
-        number = {}
+        banks = {}
 
         def take_bank(key):
-            number[key] = free_banks.pop(0)
-            return psum.tile([P, CHUNK], F32, name="bank%d" % number[key], tag="bank%d" % number[key])
+            n = free_banks.pop(0)
+            banks[key] = (n, psum.tile([P, WIDTH], F32, name="bank%d" % n, tag="bank%d" % n))
+            return banks[key][1]
 
         def give_bank(key):
-            free_banks.append(number[key])
+            free_banks.append(banks[key][0])
 
         def copy_on(engine, dst, src):
             if engine == "scalar":
@@ -53,145 +61,28 @@ def tile_district_heat_dispatch_s12_kernel(
             else:
                 nc.vector.tensor_copy(out=dst, in_=src)
 
-        def mx_tiles(name):
-            codes = keep.tile([P, CHUNK], U32, name=name + "_codes", align_bytes=64)
-            scales = keep.tile([P, CHUNK], U8, name=name + "_scales", align_bytes=64)
+        def mx_operand(name):
+            codes = keep.tile([P, WIDTH], U32, name=name + "_codes", align_bytes=64)
+            scales = keep.tile([P, WIDTH], U8, name=name + "_scales", align_bytes=64)
             return codes, scales
 
-        def quantize(planes, grouped, cols=ALL):
+        def quantize(operand, grouped, cols=ALL):
             nc.vector.quantize_mx(
-                out=planes[0][:, cols].bitcast(FP8X4),
-                scales=planes[1][:, cols],
-                in_=grouped[:, PACK * cols.start : PACK * cols.stop],
+                out=operand[0][:, cols].bitcast(FP8X4),
+                scales=operand[1][:, cols],
+                in_=grouped[:, SLOTS * cols.start : SLOTS * cols.stop],
             )
 
         def grouped_tile(name):
-            return work.tile([P, PACK * CHUNK], BF16, name=name, tag="grouped", bufs=4, align_bytes=64)
+            return work.tile([P, SLOTS * WIDTH], BF16, name=name, tag="grouped", bufs=GROUPED_BUFS, align_bytes=64)
 
-        def interleave(engine, grouped, slots, cols=ALL):
-            copy_on(
-                engine,
-                grouped[:, PACK * cols.start : PACK * cols.stop].rearrange("p (c i t) -> p c t i", i=4, t=PACK),
-                slots[:, :, cols].rearrange("p t (c i) -> p c t i", i=4),
-            )
+        def slots_tile(name):
+            return work.tile([P, SLOTS, WIDTH], BF16, name=name, tag="slots", bufs=SLOT_BUFS)
 
-        w_raw, r_raw = {}, {}
-
-        def load_weather(h):
-            w_raw[h] = keep.tile([P, 2, K], BF16, name="w_raw%d" % h, align_bytes=64)
-            nc.sync.dma_start(
-                out=w_raw[h][:], in_=weather[HALF * h : HALF * (h + 1), :].rearrange("(n e) k -> n e k", e=2)
-            )
-
-        def load_response(g, s):
-            r_raw[g, s] = keep.tile([P, PACK, PASS], BF16, name="r_raw%d%d" % (g, s))
-            nc.sync.dma_start(
-                out=r_raw[g, s][:],
-                in_=response[PASS * g : PASS * (g + 1), PASS * s : PASS * (s + 1)].rearrange("(p j) b -> p j b", j=PACK),
-            )
-
-        ident = keep.tile([P, P], F32, name="ident")
-        vec_raw = keep.tile([P, PASS], BF16, name="vec_raw")
-        site_plane_raw = keep.tile([P, B], U8, name="site_plane_raw", align_bytes=64)
-        plant_plane = keep.tile([P, NP], U8, name="plant_plane", align_bytes=64)
-        site_raw = keep.tile([P, 2 * B], U8, name="site_raw", align_bytes=64)
-        plant = keep.tile([P, 2 * NP], U8, name="plant", align_bytes=64)
-        warm = keep.tile([P, 1], F32, name="warm")
-
-        nc.vector.memset(site_plane_raw[:].bitcast(I32), 0)
-        nc.vector.memset(plant_plane[:].bitcast(I32), 0)
-        nc.vector.memset(vec_raw[:], 0.0)
-        nc.vector.memset(warm[:], 0.0)
-        make_identity(nc, ident[:])
-        nc.scalar.activation(out=warm[:], in_=warm[:], func=ACT.Relu)
-
-        def load_scale_row(plane, scales, r):
-            nc.sync.dma_start(out=plane[r:P:32, :].bitcast(I32), in_=scales[0, r:16:4, :].bitcast(I32))
-
-        def load_vector(row, vector):
-            nc.sync.dma_start(out=vec_raw[row : row + 2, :], in_=vector.rearrange("(s b) -> s b", s=2))
-
-        load_weather(0)
-        for r in range(4):
-            load_scale_row(site_plane_raw, site_scales, r)
-        nc.sync.dma_start(out=site_raw[:].bitcast(I32), in_=site_words[0].bitcast(I32))
-        load_response(0, 0)
-        nc.sync.dma_start(out=plant[:].bitcast(I32), in_=plant_words[0].bitcast(I32))
-        for r in range(4):
-            load_scale_row(plant_plane, plant_scales, r)
-        load_response(1, 0)
-        load_weather(1)
-        load_vector(0, base)
-        load_vector(2, cap)
-        load_response(0, 1)
-        load_response(1, 1)
-        for h in range(2, 2 * CHUNKS):
-            load_weather(h)
-
-        w_grouped, w_mx, r_grouped, r_mx = {}, {}, {}, {}
-        l_slots, l_grouped, l_mx = {}, {}, {}
-        c_slots, c_grouped, c_mx = {}, {}, {}
-        banks = {}
-        vec = keep.tile([P, PACK, 4], F32, name="vec")
-        vec_f32 = keep.tile([P, PASS], F32, name="vec_f32")
-        site = keep.tile([P, 2 * B], U8, name="site", align_bytes=64)
-        site_plane = keep.tile([P, B], U8, name="site_plane", align_bytes=64)
-
-        def turn_weather(h, g, engine):
-            c, hh = divmod(h, 2)
-            if hh == 0:
-                w_grouped[c, g] = work.tile([P, PACK * CHUNK], BF16, name="w_grouped", bufs=4, align_bytes=64)
-            bank = take_bank("turn")
-            words = w_raw[h][:].bitcast(F32)
-            for e in range(2):
-                for u in range(2):
-                    col = P * (2 * e + u)
-                    nc.tensor.transpose(bank[:, col : col + P], words[:, e, HALF * g + u : HALF * (g + 1) : 2], ident[:])
-            copy_on(
-                engine,
-                w_grouped[c, g][:].bitcast(F32)[:, CHUNK * hh : CHUNK * (hh + 1)].rearrange("p (e n u) -> p e n u", e=2, u=2),
-                bank[:].rearrange("p (e u n) -> p e n u", e=2, u=2),
-            )
-            give_bank("turn")
-
-        def quantize_weather(c, g, cols=ALL):
-            if (c, g) not in w_mx:
-                w_mx[c, g] = mx_tiles("w%d%d" % (c, g))
-            quantize(w_mx[c, g], w_grouped[c, g], cols)
-
-        def group_response(g, s, engine):
-            r_grouped[g, s] = grouped_tile("r_grouped")
-            copy_on(
-                engine,
-                r_grouped[g, s][:].rearrange("p (t m r j) -> p t m j r", t=PACK, r=4, j=PACK),
-                r_raw[g, s][:].rearrange("p j (m t r) -> p t m j r", t=PACK, r=4),
-            )
-
-        def quantize_response(g, s):
-            r_mx[g, s] = mx_tiles("r%d%d" % (g, s))
-            quantize(r_mx[g, s], r_grouped[g, s])
-
-        def widen_vectors():
+        def interleave(grouped, slots, cols=ALL):
             nc.vector.tensor_copy(
-                out=vec_f32[:].rearrange("p (t m r) -> p t m r", t=PACK, r=4),
-                in_=vec_raw[:].rearrange("p (m t r) -> p t m r", t=PACK, r=4),
-            )
-
-        def turn_vectors():
-            bank = take_bank("vec")
-            for t in range(PACK):
-                nc.tensor.transpose(bank[:, P * t : P * (t + 1)], vec_f32[:, P * t : P * (t + 1)], ident[:])
-            nc.scalar.copy(out=vec[:], in_=bank[:].rearrange("p (t n) -> p t n", t=PACK)[:, :, 0:4])
-            give_bank("vec")
-
-        def order_site():
-            nc.vector.tensor_copy(
-                out=site[:].bitcast(I32).rearrange("p (s t m w) -> p s t m w", s=2, t=PACK, w=2),
-                in_=site_raw[:].bitcast(I32).rearrange("p (s m t w) -> p s t m w", s=2, t=PACK, w=2),
-            )
-            nc.vector.tensor_copy(
-                out=site_plane[:].bitcast(I32).rearrange("p (s t m) -> p s t m", s=2, t=PACK),
-                in_=site_plane_raw[:].bitcast(I32).rearrange("p (s m t) -> p s t m", s=2, t=PACK),
+                out=grouped[:, SLOTS * cols.start : SLOTS * cols.stop].rearrange("p (c i t) -> p c t i", i=4, t=SLOTS),
+                in_=slots[:, :, cols].rearrange("p t (c i) -> p c t i", i=4),
             )
 
         def mx_pass(acc, stationary, j, moving, cols, start, stop):
@@ -206,204 +97,327 @@ def tile_district_heat_dispatch_s12_kernel(
                 stop=stop,
             )
 
-        def load_pass(c, s, t, g, cols=ALL, new_bank=True):
-            if g == 0 and new_bank:
-                banks["l", t] = take_bank(("l", t))
-            mx_pass(banks["l", t][:, cols], r_mx[g, s], t, w_mx[c, g], cols, g == 0, g == 1)
+        ident = keep.tile([P, P], F32, name="ident")
+        vec_rows = keep.tile([P, PASS], BF16, name="vec_rows")
+        site_scales_raw = keep.tile([P, B], U8, name="site_scales_raw", align_bytes=64)
+        plant_scales_sb = keep.tile([P, PLANTS], U8, name="plant_scales_sb", align_bytes=64)
+        site_words_raw = keep.tile([P, 2 * B], U8, name="site_words_raw", align_bytes=64)
+        plant_words_sb = keep.tile([P, 2 * PLANTS], U8, name="plant_words_sb", align_bytes=64)
 
-        def relu_out(c, s, t, engine, cols=ALL):
-            if (c, s) not in l_slots:
-                l_slots[c, s] = work.tile([P, PACK, CHUNK], BF16, name="l_slots", tag="slots", bufs=6)
-            bias = vec[:, t, s : s + 1]
-            row = l_slots[c, s][:, t, cols]
-            if engine == "scalar":
-                nc.scalar.activation(out=row, in_=banks["l", t][:, cols], func=ACT.Relu, bias=bias)
-            else:
-                nc.vector.tensor_scalar(
-                    out=row, in0=banks["l", t][:, cols], scalar1=bias, scalar2=0.0, op0=ALU.add, op1=ALU.max
-                )
-            give_bank(("l", t))
+        nc.vector.memset(site_scales_raw[:].bitcast(I32), 0)
+        nc.vector.memset(plant_scales_sb[:].bitcast(I32), 0)
+        nc.vector.memset(vec_rows[:], 0.0)
+        make_identity(nc, ident[:])
 
-        def loads(c, s, t, engine="scalar", cols=ALL):
-            for g in range(2):
-                load_pass(c, s, t, g, cols)
-            relu_out(c, s, t, engine, cols)
+        w_raw, r_raw = {}, {}
 
-        def clip(c, s, t, cols=ALL):
-            row = l_slots[c, s][:, t, cols]
-            nc.vector.tensor_scalar(
-                out=row, in0=row, scalar1=vec[:, t, 2 + s : 3 + s], scalar2=None, op0=ALU.min
+        def load_weather(h):
+            w_raw[h] = keep.tile([P, 2, K], BF16, name="w_raw%d" % h, align_bytes=64)
+            nc.sync.dma_start(
+                out=w_raw[h][:], in_=weather[HALF * h : HALF * (h + 1), :].rearrange("(n e) k -> n e k", e=2)
             )
 
-        def group_load(c, s, cols=ALL):
-            if (c, s) not in l_grouped:
-                l_grouped[c, s] = grouped_tile("l_grouped")
-            interleave("vector", l_grouped[c, s], l_slots[c, s], cols)
+        def load_response(g, s):
+            r_raw[g, s] = keep.tile([P, SLOTS, PASS], BF16, name="r_raw%d%d" % (g, s))
+            piece = response[PASS * g : PASS * (g + 1), PASS * s : PASS * (s + 1)]
+            nc.sync.dma_start(out=r_raw[g, s][:], in_=piece.rearrange("(p j) b -> p j b", j=SLOTS))
 
-        def quantize_load(c, s, cols=ALL):
-            if (c, s) not in l_mx:
-                l_mx[c, s] = mx_tiles("l%d%d" % (c, s))
-            quantize(l_mx[c, s], l_grouped[c, s], cols)
+        def load_scale_rows(scales_sb, scales):
+            for r in range(4):
+                nc.sync.dma_start(
+                    out=scales_sb[r:P:QUADRANT, :].bitcast(I32), in_=scales[0, r:SCALE_ROWS:4, :].bitcast(I32)
+                )
 
-        def coefficient_pass(s, t):
-            i = PACK * s + t
-            banks["c", i] = take_bank(("c", i))
+        def load_vector(row, vector):
+            nc.sync.dma_start(out=vec_rows[row : row + 2, :], in_=vector.rearrange("(s b) -> s b", s=2))
+
+        load_weather(0)
+        load_scale_rows(site_scales_raw, site_scales)
+        nc.sync.dma_start(out=site_words_raw[:].bitcast(I32), in_=site_words[0].bitcast(I32))
+        load_response(0, 0)
+        nc.sync.dma_start(out=plant_words_sb[:].bitcast(I32), in_=plant_words[0].bitcast(I32))
+        load_scale_rows(plant_scales_sb, plant_scales)
+        load_response(1, 0)
+        load_weather(1)
+        load_vector(0, base)
+        load_vector(2, cap)
+        load_response(0, 1)
+        load_response(1, 1)
+        for h in range(2, T // HALF):
+            load_weather(h)
+
+        w_turned, w_mx = {}, {}
+
+        def turn_half(c, h, g, engine="scalar"):
+            if h == 0:
+                w_turned[c, g] = work.tile([P, SLOTS * WIDTH], BF16, name="w_turned", bufs=TURNED_BUFS, align_bytes=64)
+            bank = take_bank("turn")
+            words = w_raw[2 * c + h][:].bitcast(F32)
+            pass_words = PASS // 2
+            for e in range(2):
+                for u in range(2):
+                    col = P * (2 * e + u)
+                    picked = words[:, e, pass_words * g + u : pass_words * (g + 1) : 2]
+                    nc.tensor.transpose(bank[:, col : col + P], picked, ident[:])
+            half_words = w_turned[c, g][:].bitcast(F32)[:, 2 * HALF * h : 2 * HALF * (h + 1)]
+            copy_on(
+                engine,
+                half_words.rearrange("p (e n u) -> p e n u", e=2, u=2),
+                bank[:].rearrange("p (e u n) -> p e n u", e=2, u=2),
+            )
+            give_bank("turn")
+
+        def turn_pass(c, g, second_engine="scalar"):
+            turn_half(c, 0, g)
+            turn_half(c, 1, g, second_engine)
+
+        def quantize_weather(c, g, cols=ALL):
+            if (c, g) not in w_mx:
+                w_mx[c, g] = mx_operand("w%d%d" % (c, g))
+            quantize(w_mx[c, g], w_turned[c, g], cols)
+
+        r_grouped, r_mx = {}, {}
+
+        def group_response(g, s):
+            r_grouped[g, s] = grouped_tile("r_grouped")
+            nc.vector.tensor_copy(
+                out=r_grouped[g, s][:].rearrange("p (t m r j) -> p t m j r", t=SLOTS, r=RUN, j=SLOTS),
+                in_=r_raw[g, s][:].rearrange("p j (m t r) -> p t m j r", t=SLOTS, r=RUN),
+            )
+
+        def quantize_response(g, s):
+            r_mx[g, s] = mx_operand("r%d%d" % (g, s))
+            quantize(r_mx[g, s], r_grouped[g, s])
+
+        vec = keep.tile([P, SLOTS, 4], F32, name="vec")
+        vec_wide = keep.tile([P, PASS], F32, name="vec_wide")
+
+        def widen_vectors():
+            nc.vector.tensor_copy(
+                out=vec_wide[:].rearrange("p (t m r) -> p t m r", t=SLOTS, r=RUN),
+                in_=vec_rows[:].rearrange("p (m t r) -> p t m r", t=SLOTS, r=RUN),
+            )
+
+        def turn_vectors():
+            bank = take_bank("vec")
+            for t in range(SLOTS):
+                nc.tensor.transpose(bank[:, P * t : P * (t + 1)], vec_wide[:, P * t : P * (t + 1)], ident[:])
+            nc.scalar.copy(out=vec[:], in_=bank[:].rearrange("p (t n) -> p t n", t=SLOTS)[:, :, 0:4])
+            give_bank("vec")
+
+        site_words_sb = keep.tile([P, 2 * B], U8, name="site_words_sb", align_bytes=64)
+        site_scales_sb = keep.tile([P, B], U8, name="site_scales_sb", align_bytes=64)
+        c_slots, c_grouped, c_mx = {}, {}, {}
+
+        def order_site():
+            nc.vector.tensor_copy(
+                out=site_words_sb[:].bitcast(I32).rearrange("p (s t m w) -> p s t m w", s=2, t=SLOTS, w=2),
+                in_=site_words_raw[:].bitcast(I32).rearrange("p (s m t w) -> p s t m w", s=2, t=SLOTS, w=2),
+            )
+            nc.vector.tensor_copy(
+                out=site_scales_sb[:].bitcast(I32).rearrange("p (s t m) -> p s t m", s=2, t=SLOTS),
+                in_=site_scales_raw[:].bitcast(I32).rearrange("p (s m t) -> p s t m", s=2, t=SLOTS),
+            )
+
+        def coef_pass(i):
             nc.tensor.matmul_mx(
-                out=banks["c", i][:],
-                lhsT=site[:, 2 * P * i : 2 * P * (i + 1)].bitcast(FP4X4),
-                lhsT_scale=site_plane[:, P * i : P * (i + 1)],
-                rhs=plant[:].bitcast(FP4X4),
-                rhs_scale=plant_plane[:],
+                out=take_bank(("coef", i))[:],
+                lhsT=site_words_sb[:, 2 * P * i : 2 * P * (i + 1)].bitcast(FP4X4),
+                lhsT_scale=site_scales_sb[:, P * i : P * (i + 1)],
+                rhs=plant_words_sb[:].bitcast(FP4X4),
+                rhs_scale=plant_scales_sb[:],
                 start=True,
                 stop=True,
             )
 
-        def coefficient_out(s, t, engine):
+        def coef_out(i, engine="scalar"):
+            s, t = divmod(i, SLOTS)
             if t == 0:
-                c_slots[s] = work.tile([P, PACK, NP], BF16, name="c_slots", tag="slots", bufs=6)
-            copy_on(engine, c_slots[s][:, t, :], banks["c", PACK * s + t][:])
-            give_bank(("c", PACK * s + t))
+                c_slots[s] = slots_tile("c_slots")
+            bank = banks["coef", i][1]
+            if engine == "scalar":
+                nc.scalar.activation(out=c_slots[s][:, t, :], in_=bank[:], func=ACT.Copy)
+            else:
+                nc.vector.tensor_copy(out=c_slots[s][:, t, :], in_=bank[:])
+            give_bank(("coef", i))
 
-        def group_coefficients(s):
+        def group_coef(s):
             c_grouped[s] = grouped_tile("c_grouped")
-            interleave("vector", c_grouped[s], c_slots[s])
+            interleave(c_grouped[s], c_slots[s])
 
-        def quantize_coefficients(s):
-            c_mx[s] = mx_tiles("c%d" % s)
+        def quantize_coef(s):
+            c_mx[s] = mx_operand("c%d" % s)
             quantize(c_mx[s], c_grouped[s])
+
+        h_slots, h_grouped, h_mx = {}, {}, {}
+
+        def heat_pass(c, s, t, g, cols=ALL):
+            if g == 0:
+                take_bank(("heat", t))
+            mx_pass(banks["heat", t][1][:, cols], r_mx[g, s], t, w_mx[c, g], cols, g == 0, g == 1)
+
+        def heat_out(c, s, t, cols=ALL):
+            if (c, s) not in h_slots:
+                h_slots[c, s] = slots_tile("h_slots")
+            nc.scalar.activation(
+                out=h_slots[c, s][:, t, cols],
+                in_=banks["heat", t][1][:, cols],
+                func=ACT.Relu,
+                bias=vec[:, t, s : s + 1],
+            )
+            give_bank(("heat", t))
+
+        def heat(c, s, cols=ALL):
+            for t in range(SLOTS):
+                for g in range(2):
+                    heat_pass(c, s, t, g, cols)
+                heat_out(c, s, t, cols)
+
+        def clip(c, s, cols=ALL):
+            for t in range(SLOTS):
+                row = h_slots[c, s][:, t, cols]
+                nc.vector.tensor_scalar(
+                    out=row, in0=row, scalar1=vec[:, t, 2 + s : 3 + s], scalar2=None, op0=ALU.min
+                )
+
+        def group_heat(c, s, cols=ALL):
+            if (c, s) not in h_grouped:
+                h_grouped[c, s] = grouped_tile("h_grouped")
+            interleave(h_grouped[c, s], h_slots[c, s], cols)
+
+        def quantize_heat(c, s, cols=ALL):
+            if (c, s) not in h_mx:
+                h_mx[c, s] = mx_operand("h%d%d" % (c, s))
+            quantize(h_mx[c, s], h_grouped[c, s], cols)
 
         def plant_pass(c, j, s):
             if s == 0:
-                banks["o", j] = take_bank(("o", j))
-            mx_pass(banks["o", j][:], l_mx[c, s], j, c_mx[s], ALL, s == 0, s == 1)
+                take_bank(("out", j))
+            mx_pass(banks["out", j][1][:], h_mx[c, s], j, c_mx[s], ALL, s == 0, s == 1)
 
-        def store(c, j, engine):
-            hh, e = divmod(j, 2)
-            result = work.tile([P, NP], F32, name="result", bufs=8)
-            copy_on(engine, result[:], banks["o", j][:])
-            give_bank(("o", j))
-            rows = out[CHUNK * c + HALF * hh : CHUNK * c + HALF * (hh + 1), :].rearrange("(n e) q -> n e q", e=2)
-            nc.sync.dma_start(out=rows[:, e, :], in_=result[:])
+        def store(c, j, engine="scalar"):
+            h, e = divmod(j, 2)
+            result = work.tile([P, PLANTS], F32, name="result", bufs=RESULT_BUFS)
+            copy_on(engine, result[:], banks["out", j][1][:])
+            give_bank(("out", j))
+            hours = out[WIDTH * c + HALF * h : WIDTH * c + HALF * (h + 1), :].rearrange("(n e) q -> n e q", e=2)
+            nc.sync.dma_start(out=hours[:, e, :], in_=result[:])
 
-        def plants(c, j, engine):
+        def plants(c, j, engine="scalar"):
             for s in range(2):
                 plant_pass(c, j, s)
             store(c, j, engine)
 
-        def turn_pass(c, g, second="scalar"):
-            turn_weather(2 * c, g, "scalar")
-            turn_weather(2 * c + 1, g, second)
 
         for g in range(2):
-            turn_weather(0, g, "scalar")
+            turn_half(0, 0, g)
         order_site()
-        quantize_weather(0, 0, HALVES[0])
-        group_response(0, 0, "vector")
-        quantize_weather(0, 1, HALVES[0])
-        for t in range(PACK):
-            coefficient_pass(0, t)
-        for t in range(2):
-            coefficient_pass(1, t)
+        quantize_weather(0, 0, FIRST)
+        group_response(0, 0)
+        quantize_weather(0, 1, FIRST)
+        early_coef = BANKS - 2
+        for i in range(early_coef):
+            coef_pass(i)
         quantize_response(0, 0)
-        group_response(1, 0, "vector")
+        group_response(1, 0)
         quantize_response(1, 0)
-        for t in range(PACK):
-            coefficient_out(0, t, "scalar")
-        coefficient_out(1, 0, "vector")
+        for i in range(SLOTS):
+            coef_out(i)
+        coef_out(SLOTS, "vector")
         widen_vectors()
         for g in range(2):
-            turn_weather(1, g, "scalar")
-        quantize_weather(0, 0, HALVES[1])
-        quantize_weather(0, 1, HALVES[1])
-        group_response(0, 1, "vector")
-        for t in range(2, PACK):
-            coefficient_pass(1, t)
+            turn_half(0, 1, g)
+        for g in range(2):
+            quantize_weather(0, g, SECOND)
+        group_response(0, 1)
+        for i in range(early_coef, 2 * SLOTS):
+            coef_pass(i)
         turn_vectors()
-        for t in range(1, PACK):
-            coefficient_out(1, t, "scalar")
-        for t in range(PACK):
-            load_pass(0, 0, t, 0)
-        group_response(1, 1, "vector")
-        quantize_response(0, 1)
-        quantize_response(1, 1)
+        for i in range(SLOTS + 1, 2 * SLOTS):
+            coef_out(i)
 
-        def load_group(c, s, ts, cols=ALL):
-            for t in ts:
-                loads(c, s, t, cols=cols)
-
-        def clips(c, s, ts, cols=ALL):
-            for t in ts:
-                clip(c, s, t, cols)
-
-        group_coefficients(0)
-        for t in range(PACK):
-            load_pass(0, 0, t, 1)
-            relu_out(0, 0, t, "scalar")
+        for t in range(SLOTS):
+            heat_pass(0, 0, t, 0)
+        group_response(1, 1)
+        for g in range(2):
+            quantize_response(g, 1)
+        group_coef(0)
+        for t in range(SLOTS):
+            heat_pass(0, 0, t, 1)
+            heat_out(0, 0, t)
         turn_pass(1, 0)
-        for t in range(PACK):
-            load_pass(0, 1, t, 0)
+        for t in range(SLOTS):
+            heat_pass(0, 1, t, 0)
         turn_pass(1, 1)
-        for t in range(PACK):
-            load_pass(0, 1, t, 1)
-            relu_out(0, 1, t, "scalar")
-        clips(0, 0, range(PACK))
+        for t in range(SLOTS):
+            heat_pass(0, 1, t, 1)
+            heat_out(0, 1, t)
+        clip(0, 0)
         quantize_weather(1, 0)
-        group_coefficients(1)
+        group_coef(1)
         quantize_weather(1, 1)
-        group_load(0, 0)
-        quantize_coefficients(0)
-        clips(0, 1, range(PACK))
-        quantize_load(0, 0)
-        group_load(0, 1)
-        quantize_coefficients(1)
-        quantize_load(0, 1)
+        group_heat(0, 0)
+        quantize_coef(0)
+        clip(0, 1)
+        quantize_heat(0, 0)
+        group_heat(0, 1)
+        quantize_coef(1)
+        quantize_heat(0, 1)
 
-        last = CHUNKS - 1
-        for c in range(1, last):
-            turn_pass(c + 1, 0, "vector" if c == 2 else "scalar")
-            if c == 2:
-                group_load(c - 1, 1)
-                quantize_weather(c + 1, 0)
-                quantize_load(c - 1, 1)
-            load_group(c, 0, range(PACK))
-            clips(c, 0, range(PACK))
-            turn_pass(c + 1, 1)
-            load_group(c, 1, range(PACK))
-            if c == 1:
-                quantize_weather(c + 1, 0)
-            group_load(c, 0)
-            quantize_weather(c + 1, 1)
-            quantize_load(c, 0)
-            clips(c, 1, range(PACK))
-            if c == 2:
-                load_group(last, 0, range(PACK))
-                group_load(c, 1)
-                clips(last, 0, range(PACK))
-                quantize_load(c, 1)
-                group_load(last, 0)
-            for j in range(4):
-                plants(c - 1, j, "vector" if c == 2 and j == 3 else "scalar")
-        c = last
-        quantize_load(c, 0)
-        load_group(c, 1, range(PACK), HALVES[0])
-        clips(c, 1, range(PACK), HALVES[0])
-        group_load(c, 1, HALVES[0])
+        for s in range(2):
+            turn_pass(2, s)
+            heat(1, s)
+        clip(1, 0)
+        quantize_weather(2, 0)
+        group_heat(1, 0)
+        quantize_weather(2, 1)
+        clip(1, 1)
+        quantize_heat(1, 0)
+        group_heat(1, 1)
+        for j in range(4):
+            plants(0, j)
+
+        turn_pass(3, 0, "vector")
+        heat(2, 0)
+        turn_pass(3, 1)
+        heat(2, 1)
+        quantize_weather(3, 0)
+        clip(2, 0)
+        quantize_heat(1, 1)
+        group_heat(2, 0)
+        quantize_weather(3, 1)
+        clip(2, 1)
+        quantize_heat(2, 0)
+        group_heat(2, 1)
+        plants(1, 0)
+        plants(1, 1, "vector")
+        heat(3, 0)
+        clip(3, 0)
+        quantize_heat(2, 1)
+        group_heat(3, 0)
+        plants(1, 2)
+        plants(1, 3)
+
+        heat(3, 1, FIRST)
+        clip(3, 1, FIRST)
+        quantize_heat(3, 0)
+        group_heat(3, 1, FIRST)
         for j in range(2):
             for s in range(2):
-                plant_pass(c - 1, j, s)
-        store(c - 1, 0, "scalar")
-        store(c - 1, 1, "vector")
-        load_group(c, 1, range(PACK), HALVES[1])
-        clips(c, 1, range(PACK), HALVES[1])
-        quantize_load(c, 1, HALVES[0])
-        group_load(c, 1, HALVES[1])
-        quantize_load(c, 1, HALVES[1])
-        for j in range(2, 4):
-            plants(c - 1, j, "scalar")
-        for j in range(2):
-            plants(c, j, "scalar")
+                plant_pass(2, j, s)
+        store(2, 0)
+        heat(3, 1, SECOND)
+        store(2, 1)
+        clip(3, 1, SECOND)
+        quantize_heat(3, 1, FIRST)
+        group_heat(3, 1, SECOND)
+        quantize_heat(3, 1, SECOND)
+        plants(2, 2)
+        plants(2, 3)
+        plants(3, 0)
+        plants(3, 1)
         for s in range(2):
-            for j in range(2, 4):
-                plant_pass(c, j, s)
-        store(c, 2, "vector")
-        store(c, 3, "scalar")
+            for j in (2, 3):
+                plant_pass(3, j, s)
+        store(3, 2, "vector")
+        store(3, 3)

from contextlib import ExitStack

import concourse.mybir as mybir
from concourse.masks import make_identity

T, K, B, A, PLANTS = 2048, 1024, 1024, 512, 512
FLOPS = 2 * T * K * B + 2 * A * B * PLANTS + 2 * T * B * PLANTS

F32 = mybir.dt.float32
BF16 = mybir.dt.bfloat16
U32 = mybir.dt.uint32
I32 = mybir.dt.int32
U8 = mybir.dt.uint8
FP8X4 = mybir.dt.float8_e4m3fn_x4
FP4X4 = mybir.dt.float4_e2m1fn_x4
ALU = mybir.AluOpType
ACT = mybir.ActivationFunctionType

P = 128
SLOTS = 4
PASS = P * SLOTS
RUN = 4
WIDTH = 512
HALF = WIDTH // 2
BANKS = 8
ALL = slice(0, WIDTH)
FIRST, SECOND = slice(0, HALF), slice(HALF, WIDTH)
SCALE_ROWS = 16
QUADRANT = 32

TURNED_BUFS = 4
GROUPED_BUFS = 4
SLOT_BUFS = 6
RESULT_BUFS = 8


def tile_district_heat_dispatch_s12_kernel(
    tc, weather, response, base, cap, site_words, site_scales, plant_words, plant_scales, out
):
    nc = tc.nc
    with ExitStack() as ctx:
        keep = ctx.enter_context(tc.tile_pool(name="keep", bufs=1))
        work = ctx.enter_context(tc.tile_pool(name="work", bufs=1))
        psum = ctx.enter_context(tc.psum_pool(name="psum", bufs=1))
        ctx.enter_context(tc.manual_schedule())

        free_banks = list(range(BANKS))
        banks = {}

        def take_bank(key):
            n = free_banks.pop(0)
            banks[key] = (n, psum.tile([P, WIDTH], F32, name="bank%d" % n, tag="bank%d" % n))
            return banks[key][1]

        def give_bank(key):
            free_banks.append(banks[key][0])

        def copy_on(engine, dst, src):
            if engine == "scalar":
                nc.scalar.copy(out=dst, in_=src)
            else:
                nc.vector.tensor_copy(out=dst, in_=src)

        def mx_operand(name):
            codes = keep.tile([P, WIDTH], U32, name=name + "_codes", align_bytes=64)
            scales = keep.tile([P, WIDTH], U8, name=name + "_scales", align_bytes=64)
            return codes, scales

        def quantize(operand, grouped, cols=ALL):
            nc.vector.quantize_mx(
                out=operand[0][:, cols].bitcast(FP8X4),
                scales=operand[1][:, cols],
                in_=grouped[:, SLOTS * cols.start : SLOTS * cols.stop],
            )

        def grouped_tile(name):
            return work.tile([P, SLOTS * WIDTH], BF16, name=name, tag="grouped", bufs=GROUPED_BUFS, align_bytes=64)

        def slots_tile(name):
            return work.tile([P, SLOTS, WIDTH], BF16, name=name, tag="slots", bufs=SLOT_BUFS)

        def interleave(grouped, slots, cols=ALL):
            nc.vector.tensor_copy(
                out=grouped[:, SLOTS * cols.start : SLOTS * cols.stop].rearrange("p (c i t) -> p c t i", i=4, t=SLOTS),
                in_=slots[:, :, cols].rearrange("p t (c i) -> p c t i", i=4),
            )

        def mx_pass(acc, stationary, j, moving, cols, start, stop):
            own = slice(P * j, P * (j + 1))
            nc.tensor.matmul_mx(
                out=acc,
                lhsT=stationary[0][:, own].bitcast(FP8X4),
                lhsT_scale=stationary[1][:, own],
                rhs=moving[0][:, cols].bitcast(FP8X4),
                rhs_scale=moving[1][:, cols],
                start=start,
                stop=stop,
            )

        ident = keep.tile([P, P], F32, name="ident")
        vec_rows = keep.tile([P, PASS], BF16, name="vec_rows")
        site_scales_raw = keep.tile([P, B], U8, name="site_scales_raw", align_bytes=64)
        plant_scales_sb = keep.tile([P, PLANTS], U8, name="plant_scales_sb", align_bytes=64)
        site_words_raw = keep.tile([P, 2 * B], U8, name="site_words_raw", align_bytes=64)
        plant_words_sb = keep.tile([P, 2 * PLANTS], U8, name="plant_words_sb", align_bytes=64)

        nc.vector.memset(site_scales_raw[:].bitcast(I32), 0)
        nc.vector.memset(plant_scales_sb[:].bitcast(I32), 0)
        nc.vector.memset(vec_rows[:], 0.0)
        make_identity(nc, ident[:])

        w_raw, r_raw = {}, {}

        def load_weather(h):
            w_raw[h] = keep.tile([P, 2, K], BF16, name="w_raw%d" % h, align_bytes=64)
            nc.sync.dma_start(
                out=w_raw[h][:], in_=weather[HALF * h : HALF * (h + 1), :].rearrange("(n e) k -> n e k", e=2)
            )

        def load_response(g, s):
            r_raw[g, s] = keep.tile([P, SLOTS, PASS], BF16, name="r_raw%d%d" % (g, s))
            piece = response[PASS * g : PASS * (g + 1), PASS * s : PASS * (s + 1)]
            nc.sync.dma_start(out=r_raw[g, s][:], in_=piece.rearrange("(p j) b -> p j b", j=SLOTS))

        def load_scale_rows(scales_sb, scales):
            for r in range(4):
                nc.sync.dma_start(
                    out=scales_sb[r:P:QUADRANT, :].bitcast(I32), in_=scales[0, r:SCALE_ROWS:4, :].bitcast(I32)
                )

        def load_vector(row, vector):
            nc.sync.dma_start(out=vec_rows[row : row + 2, :], in_=vector.rearrange("(s b) -> s b", s=2))

        load_weather(0)
        load_scale_rows(site_scales_raw, site_scales)
        nc.sync.dma_start(out=site_words_raw[:].bitcast(I32), in_=site_words[0].bitcast(I32))
        load_response(0, 0)
        nc.sync.dma_start(out=plant_words_sb[:].bitcast(I32), in_=plant_words[0].bitcast(I32))
        load_scale_rows(plant_scales_sb, plant_scales)
        load_response(1, 0)
        load_weather(1)
        load_vector(0, base)
        load_vector(2, cap)
        load_response(0, 1)
        load_response(1, 1)
        for h in range(2, T // HALF):
            load_weather(h)

        w_turned, w_mx = {}, {}

        def turn_half(c, h, g, engine="scalar"):
            if h == 0:
                w_turned[c, g] = work.tile([P, SLOTS * WIDTH], BF16, name="w_turned", bufs=TURNED_BUFS, align_bytes=64)
            bank = take_bank("turn")
            words = w_raw[2 * c + h][:].bitcast(F32)
            pass_words = PASS // 2
            for e in range(2):
                for u in range(2):
                    col = P * (2 * e + u)
                    picked = words[:, e, pass_words * g + u : pass_words * (g + 1) : 2]
                    nc.tensor.transpose(bank[:, col : col + P], picked, ident[:])
            half_words = w_turned[c, g][:].bitcast(F32)[:, 2 * HALF * h : 2 * HALF * (h + 1)]
            copy_on(
                engine,
                half_words.rearrange("p (e n u) -> p e n u", e=2, u=2),
                bank[:].rearrange("p (e u n) -> p e n u", e=2, u=2),
            )
            give_bank("turn")

        def turn_pass(c, g, second_engine="scalar"):
            turn_half(c, 0, g)
            turn_half(c, 1, g, second_engine)

        def quantize_weather(c, g, cols=ALL):
            if (c, g) not in w_mx:
                w_mx[c, g] = mx_operand("w%d%d" % (c, g))
            quantize(w_mx[c, g], w_turned[c, g], cols)

        r_grouped, r_mx = {}, {}

        def group_response(g, s):
            r_grouped[g, s] = grouped_tile("r_grouped")
            nc.vector.tensor_copy(
                out=r_grouped[g, s][:].rearrange("p (t m r j) -> p t m j r", t=SLOTS, r=RUN, j=SLOTS),
                in_=r_raw[g, s][:].rearrange("p j (m t r) -> p t m j r", t=SLOTS, r=RUN),
            )

        def quantize_response(g, s):
            r_mx[g, s] = mx_operand("r%d%d" % (g, s))
            quantize(r_mx[g, s], r_grouped[g, s])

        vec = keep.tile([P, SLOTS, 4], F32, name="vec")
        vec_wide = keep.tile([P, PASS], F32, name="vec_wide")

        def widen_vectors():
            nc.vector.tensor_copy(
                out=vec_wide[:].rearrange("p (t m r) -> p t m r", t=SLOTS, r=RUN),
                in_=vec_rows[:].rearrange("p (m t r) -> p t m r", t=SLOTS, r=RUN),
            )

        def turn_vectors():
            bank = take_bank("vec")
            for t in range(SLOTS):
                nc.tensor.transpose(bank[:, P * t : P * (t + 1)], vec_wide[:, P * t : P * (t + 1)], ident[:])
            nc.scalar.copy(out=vec[:], in_=bank[:].rearrange("p (t n) -> p t n", t=SLOTS)[:, :, 0:4])
            give_bank("vec")

        site_words_sb = keep.tile([P, 2 * B], U8, name="site_words_sb", align_bytes=64)
        site_scales_sb = keep.tile([P, B], U8, name="site_scales_sb", align_bytes=64)
        c_slots, c_grouped, c_mx = {}, {}, {}

        def order_site():
            nc.vector.tensor_copy(
                out=site_words_sb[:].bitcast(I32).rearrange("p (s t m w) -> p s t m w", s=2, t=SLOTS, w=2),
                in_=site_words_raw[:].bitcast(I32).rearrange("p (s m t w) -> p s t m w", s=2, t=SLOTS, w=2),
            )
            nc.vector.tensor_copy(
                out=site_scales_sb[:].bitcast(I32).rearrange("p (s t m) -> p s t m", s=2, t=SLOTS),
                in_=site_scales_raw[:].bitcast(I32).rearrange("p (s m t) -> p s t m", s=2, t=SLOTS),
            )

        def coef_pass(i):
            nc.tensor.matmul_mx(
                out=take_bank(("coef", i))[:],
                lhsT=site_words_sb[:, 2 * P * i : 2 * P * (i + 1)].bitcast(FP4X4),
                lhsT_scale=site_scales_sb[:, P * i : P * (i + 1)],
                rhs=plant_words_sb[:].bitcast(FP4X4),
                rhs_scale=plant_scales_sb[:],
                start=True,
                stop=True,
            )

        def coef_out(i, engine="scalar"):
            s, t = divmod(i, SLOTS)
            if t == 0:
                c_slots[s] = slots_tile("c_slots")
            bank = banks["coef", i][1]
            if engine == "scalar":
                nc.scalar.activation(out=c_slots[s][:, t, :], in_=bank[:], func=ACT.Copy)
            else:
                nc.vector.tensor_copy(out=c_slots[s][:, t, :], in_=bank[:])
            give_bank(("coef", i))

        def group_coef(s):
            c_grouped[s] = grouped_tile("c_grouped")
            interleave(c_grouped[s], c_slots[s])

        def quantize_coef(s):
            c_mx[s] = mx_operand("c%d" % s)
            quantize(c_mx[s], c_grouped[s])

        h_slots, h_grouped, h_mx = {}, {}, {}

        def heat_pass(c, s, t, g, cols=ALL):
            if g == 0:
                take_bank(("heat", t))
            mx_pass(banks["heat", t][1][:, cols], r_mx[g, s], t, w_mx[c, g], cols, g == 0, g == 1)

        def heat_out(c, s, t, cols=ALL):
            if (c, s) not in h_slots:
                h_slots[c, s] = slots_tile("h_slots")
            nc.scalar.activation(
                out=h_slots[c, s][:, t, cols],
                in_=banks["heat", t][1][:, cols],
                func=ACT.Relu,
                bias=vec[:, t, s : s + 1],
            )
            give_bank(("heat", t))

        def heat(c, s, cols=ALL):
            for t in range(SLOTS):
                for g in range(2):
                    heat_pass(c, s, t, g, cols)
                heat_out(c, s, t, cols)

        def clip(c, s, cols=ALL):
            for t in range(SLOTS):
                row = h_slots[c, s][:, t, cols]
                nc.vector.tensor_scalar(
                    out=row, in0=row, scalar1=vec[:, t, 2 + s : 3 + s], scalar2=None, op0=ALU.min
                )

        def group_heat(c, s, cols=ALL):
            if (c, s) not in h_grouped:
                h_grouped[c, s] = grouped_tile("h_grouped")
            interleave(h_grouped[c, s], h_slots[c, s], cols)

        def quantize_heat(c, s, cols=ALL):
            if (c, s) not in h_mx:
                h_mx[c, s] = mx_operand("h%d%d" % (c, s))
            quantize(h_mx[c, s], h_grouped[c, s], cols)

        def plant_pass(c, j, s):
            if s == 0:
                take_bank(("out", j))
            mx_pass(banks["out", j][1][:], h_mx[c, s], j, c_mx[s], ALL, s == 0, s == 1)

        def store(c, j, engine="scalar"):
            h, e = divmod(j, 2)
            result = work.tile([P, PLANTS], F32, name="result", bufs=RESULT_BUFS)
            copy_on(engine, result[:], banks["out", j][1][:])
            give_bank(("out", j))
            hours = out[WIDTH * c + HALF * h : WIDTH * c + HALF * (h + 1), :].rearrange("(n e) q -> n e q", e=2)
            nc.sync.dma_start(out=hours[:, e, :], in_=result[:])

        def plants(c, j, engine="scalar"):
            for s in range(2):
                plant_pass(c, j, s)
            store(c, j, engine)


        for g in range(2):
            turn_half(0, 0, g)
        order_site()
        quantize_weather(0, 0, FIRST)
        group_response(0, 0)
        quantize_weather(0, 1, FIRST)
        early_coef = BANKS - 2
        for i in range(early_coef):
            coef_pass(i)
        quantize_response(0, 0)
        group_response(1, 0)
        quantize_response(1, 0)
        for i in range(SLOTS):
            coef_out(i)
        coef_out(SLOTS, "vector")
        widen_vectors()
        for g in range(2):
            turn_half(0, 1, g)
        for g in range(2):
            quantize_weather(0, g, SECOND)
        group_response(0, 1)
        for i in range(early_coef, 2 * SLOTS):
            coef_pass(i)
        turn_vectors()
        for i in range(SLOTS + 1, 2 * SLOTS):
            coef_out(i)

        for t in range(SLOTS):
            heat_pass(0, 0, t, 0)
        group_response(1, 1)
        for g in range(2):
            quantize_response(g, 1)
        group_coef(0)
        for t in range(SLOTS):
            heat_pass(0, 0, t, 1)
            heat_out(0, 0, t)
        turn_pass(1, 0)
        for t in range(SLOTS):
            heat_pass(0, 1, t, 0)
        turn_pass(1, 1)
        for t in range(SLOTS):
            heat_pass(0, 1, t, 1)
            heat_out(0, 1, t)
        clip(0, 0)
        quantize_weather(1, 0)
        group_coef(1)
        quantize_weather(1, 1)
        group_heat(0, 0)
        quantize_coef(0)
        clip(0, 1)
        quantize_heat(0, 0)
        group_heat(0, 1)
        quantize_coef(1)
        quantize_heat(0, 1)

        for s in range(2):
            turn_pass(2, s)
            heat(1, s)
        clip(1, 0)
        quantize_weather(2, 0)
        group_heat(1, 0)
        quantize_weather(2, 1)
        clip(1, 1)
        quantize_heat(1, 0)
        group_heat(1, 1)
        for j in range(4):
            plants(0, j)

        turn_pass(3, 0, "vector")
        heat(2, 0)
        turn_pass(3, 1)
        heat(2, 1)
        quantize_weather(3, 0)
        clip(2, 0)
        quantize_heat(1, 1)
        group_heat(2, 0)
        quantize_weather(3, 1)
        clip(2, 1)
        quantize_heat(2, 0)
        group_heat(2, 1)
        plants(1, 0)
        plants(1, 1, "vector")
        heat(3, 0)
        clip(3, 0)
        quantize_heat(2, 1)
        group_heat(3, 0)
        plants(1, 2)
        plants(1, 3)

        heat(3, 1, FIRST)
        clip(3, 1, FIRST)
        quantize_heat(3, 0)
        group_heat(3, 1, FIRST)
        for j in range(2):
            for s in range(2):
                plant_pass(2, j, s)
        store(2, 0)
        heat(3, 1, SECOND)
        store(2, 1)
        clip(3, 1, SECOND)
        quantize_heat(3, 1, FIRST)
        group_heat(3, 1, SECOND)
        quantize_heat(3, 1, SECOND)
        plants(2, 2)
        plants(2, 3)
        plants(3, 0)
        plants(3, 1)
        for s in range(2):
            for j in (2, 3):
                plant_pass(3, j, s)
        store(3, 2, "vector")
        store(3, 3)
